import numpy as np
import ml_dtypes


def mxq(x, axis, fmt="e4m3"):
    dtype, down = {"e4m3": (ml_dtypes.float8_e4m3fn, 7), "e5m2": (ml_dtypes.float8_e5m2, 14)}[fmt]
    v = np.moveaxis(np.asarray(x, np.float32).astype(ml_dtypes.bfloat16).astype(np.float64), axis, -1)
    blocks = v.reshape(v.shape[:-1] + (-1, 32))
    amax = np.abs(blocks).max(-1, keepdims=True)
    byte = np.maximum(np.where(amax > 0, np.frexp(amax)[1] - 1 + 127, 0) - down, 1)
    scale = np.exp2(byte - 127.0)
    codes = (blocks / scale).astype(np.float32).astype(dtype).astype(np.float64)
    return np.moveaxis((codes * scale).reshape(v.shape), -1, axis)


WIDE = False


def mx_kscale(k):
    if not WIDE:
        return np.ones(k)
    levels = np.array([10, -10, 5, -5, 0])
    if k % 512:
        return np.exp2(np.random.permutation(np.resize(levels, k // 32))).repeat(32)
    a = np.empty((k // 512, 16))
    for p in range(k // 512):
        a[p, :8] = np.random.permutation(np.resize(levels, 8))
        for g in range(8):
            far = levels[np.abs(levels - a[p, g]) >= 10]
            a[p, g + 8] = far[np.random.randint(len(far))]
    return np.exp2(a.ravel()).repeat(32)


def f64(x):
    return np.asarray(x).astype(np.float64)


def striped(idx):
    return np.tile(idx.reshape(-1, 16).T, (8, 1)).astype(np.uint16)


def unstriped(offs):
    return offs[:16].T.reshape(-1).astype(np.int64)


E2M1 = np.array([0.0, 0.5, 1.0, 1.5, 2.0, 3.0, 4.0, 6.0, -0.0, -0.5, -1.0, -1.5, -2.0, -3.0, -4.0, -6.0])


def pack_weight(w, fmt):
    k, n = w.shape
    w = f64(np.asarray(w, np.float32).astype(ml_dtypes.bfloat16)).reshape(k // 32, 32, n)
    amax = np.abs(w).max(1)
    if fmt == "e4m3":
        byte = np.frexp(amax)[1] - 1 + 127 - 7
    else:
        mant, ex = np.frexp(amax / 6.0)
        byte = np.where(mant > 0.5, ex, ex - 1) + 127
    byte = np.clip(np.where(amax > 0, byte, 1), 1, 254)
    scaled = (w * np.exp2(127.0 - byte)[:, None, :]).reshape(k, n).astype(np.float32)
    by_word = np.ascontiguousarray(scaled.reshape(k // 512, 128, 4, n).transpose(0, 1, 3, 2))
    if fmt == "e4m3":
        words = by_word.astype(ml_dtypes.float8_e4m3fn).view(np.uint8)
    else:
        c = by_word.astype(ml_dtypes.float4_e2m1fn).view(np.uint8) & 0xF
        words = (c[..., 0::2] | (c[..., 1::2] << 4)).reshape(k // 512, 128, 2 * n)
    return np.ascontiguousarray(words), np.ascontiguousarray(byte.astype(np.uint8).reshape(k // 512, 16, n))


def unpack_weight(words, scales, fmt):
    g, _, n = scales.shape
    words = np.ascontiguousarray(words).reshape(g, 128, n, -1)
    if fmt == "e4m3":
        vals = words.view(ml_dtypes.float8_e4m3fn).astype(np.float64)
    else:
        nib = np.empty((g, 128, n, 4), np.uint8)
        nib[..., 0::2] = words & 0xF
        nib[..., 1::2] = words >> 4
        vals = E2M1[nib]
    vals = vals * np.repeat(np.exp2(scales.astype(np.float64) - 127.0), 8, axis=1)[..., None]
    return vals.transpose(0, 1, 3, 2).reshape(g * 512, n)


def gelu(v):
    return 0.5 * v * (1.0 + np.tanh(np.sqrt(2.0 / np.pi) * (v + 0.044715 * v**3)))


def bf(x):
    return np.asarray(x, np.float32).astype(ml_dtypes.bfloat16)


def planes(Y):
    n, m = Y.shape
    b = f64(bf(Y)).reshape(n // 32, 32, m)
    amax = np.abs(b).max(1)
    byte = np.clip(np.where(amax > 0, np.frexp(amax)[1] - 1 + 127 - 7, 1), 1, 254)
    codes = (b * np.exp2(127.0 - byte)[:, None, :]).reshape(n, m).astype(np.float32).astype(ml_dtypes.float8_e4m3fn).view(np.uint8)
    words = codes.reshape(n // 512, 128, 4, m).transpose(0, 1, 3, 2)
    return np.ascontiguousarray(words), np.ascontiguousarray(byte.astype(np.uint8).reshape(n // 512, 16, m))


K, K2, T, S, H, N = 1536, 1024, 2048, 1024, 512, 1024

def setup_inputs():
    n = np.random.standard_normal
    s, s2, u = mx_kscale(K)[:, None], mx_kscale(K2)[:, None], mx_kscale(H)[:, None]
    d = {}
    d["tab_words"], d["tab_scales"] = pack_weight(n((K, T)) * s, "e4m3")
    d["offs"] = striped(np.random.permutation(T)[:S])
    d["xs_words"], d["xs_scales"] = pack_weight(n((K2, S)) * s2, "e4m3")
    d["w1"] = (n((K, H)) / s * u.T / K**0.5).astype(np.float32)
    d["bias1"] = (0.5 * n(H) * u[:, 0]).astype(np.float32)
    d["wx_words"], d["wx_scales"] = pack_weight(n((K2, H)) / s2 * u.T / K2**0.5, "e2m1")
    d["w2"] = (1.5 * n((H, H)) / u / H**0.5).astype(np.float32)
    d["bias2"] = (0.7 * n(H)).astype(np.float32)
    d["gain"] = (1.3 * np.exp(0.3 * n(H)) * u[:, 0]).astype(np.float32)
    d["w3_words"], d["w3_scales"] = pack_weight(n((H, N)) / u / H**0.5 * np.exp(0.8 * n(N)), "e2m1")
    return d

def reference(tab_words, tab_scales, offs, xs_words, xs_scales, w1, bias1, wx_words, wx_scales, w2, bias2, gain, w3_words, w3_scales):
    v = unpack_weight(tab_words, tab_scales, "e4m3")[:, unstriped(offs)]
    xs = unpack_weight(xs_words, xs_scales, "e4m3")
    wx = unpack_weight(wx_words, wx_scales, "e2m1")
    w3 = unpack_weight(w3_words, w3_scales, "e2m1")
    sea = (mxq(f64(w1), 0, "e4m3").T @ v) + f64(bias1)[:, None]
    moor = wx.T @ xs
    z = np.maximum(sea, moor)
    resp = np.tanh((mxq(f64(w2), 0, "e4m3").T @ mxq(z, 0, "e4m3")) + f64(bias2)[:, None])
    diff = f64(gain)[:, None] * resp - moor
    y = w3.T @ mxq(diff, 0, "e4m3")
    words, scales = planes(y)
    return y, words, scales

@@ -1,0 +1,355 @@
+from contextlib import ExitStack
+
+import concourse.mybir as mybir
+
+K, K2, T, S, H, N = 1536, 1024, 2048, 1024, 512, 1024
+FLOPS = 2 * S * (K * H + K2 * H + H * H + H * N)
+
+F32 = mybir.dt.float32
+BF16 = mybir.dt.bfloat16
+I32 = mybir.dt.int32
+U32 = mybir.dt.uint32
+U16 = mybir.dt.uint16
+U8 = mybir.dt.uint8
+FP8X4 = mybir.dt.float8_e4m3fn_x4
+FP4X4 = mybir.dt.float4_e2m1fn_x4
+ALU = mybir.AluOpType
+ACT = mybir.ActivationFunctionType
+
+P = 128
+PACK = 4
+PASS = P * PACK
+HALF = 512
+W = 256
+QUADS = 4
+
+
+def tile_list_buoy_damping_features_kernel(
+    tc, tab_words, tab_scales, offs, xs_words, xs_scales, w1, bias1, wx_words, wx_scales,
+    w2, bias2, gain, w3_words, w3_scales, out_0, out_1, out_2,
+):
+    nc = tc.nc
+    n_sea, n_moor, n_groups = K // PASS, K2 // PASS, N // PASS
+    halves, chunks = S // HALF, S // W
+
+    with ExitStack() as ctx:
+        keep = ctx.enter_context(tc.tile_pool(name="keep", bufs=1))
+        ring = ctx.enter_context(tc.tile_pool(name="ring", bufs=2))
+        psum = ctx.enter_context(tc.psum_pool(name="psum", bufs=8))
+
+        def held(shape, dtype, name):
+            return keep.tile(shape, dtype, name=name, align_bytes=64)
+
+        def bank(shape):
+            return psum.tile(shape, F32, name="bank")
+
+        wx_sc_raw = held([P, n_moor, H], U8, "wx_sc_raw")
+        xs_sc = held([P, n_moor, S], U8, "xs_sc")
+        tab_sc = held([P, T], U8, "tab_sc")
+        w3_sc_raw = held([P, 1, N], U8, "w3_sc_raw")
+        nc.vector.memset(tab_sc[:, :T // 2].bitcast(I32), 0)
+        nc.gpsimd.memset(tab_sc[:, T // 2:].bitcast(I32), 0)
+        nc.vector.memset(wx_sc_raw[:].bitcast(I32), 0)
+        nc.vector.memset(w3_sc_raw[:].bitcast(I32), 0)
+
+        offsets = keep.tile([P, S // 16], U16, name="offsets")
+        nc.sync.dma_start(offsets[:], offs)
+
+        tab = [held([P, T], U32, f"tab{a}") for a in range(n_sea)]
+
+        def load_tab(a):
+            nc.sync.dma_start(tab[a][:].bitcast(I32), tab_words[a].rearrange("p n i -> p (n i)").bitcast(I32))
+
+        def load_rows(w, a, c0, c1, name):
+            raw = held([P, PACK, c1 - c0], F32, name)
+            nc.sync.dma_start(raw[:], w[a * PASS:(a + 1) * PASS, c0:c1].rearrange("(p j) c -> p j c", j=PACK))
+            return raw
+
+        def load_vec(v, name):
+            col = held([P, PACK], F32, name)
+            nc.sync.dma_start(col[:], v.rearrange("(p t) -> p t", t=PACK))
+            return col
+
+        def load_planes(queue, plane, scales):
+            for q in range(QUADS):
+                queue.dma_start(
+                    plane[32 * q:32 * q + 4, :, :].bitcast(I32),
+                    scales[:, 4 * q:4 * q + 4, :].rearrange("a r n -> r a n").bitcast(I32),
+                )
+
+        load_tab(0)
+        wx_raw = held([P, n_moor, H], U16, "wx_raw")
+        nc.sync.dma_start(wx_raw[:].bitcast(I32), wx_words.rearrange("a p b -> p a b").bitcast(I32))
+        load_planes(nc.sync, xs_sc, xs_scales)
+        load_tab(1)
+        b1 = load_vec(bias1, "b1")
+        b2 = load_vec(bias2, "b2")
+        gn = load_vec(gain, "gn")
+        w3_raw = held([P, N], U16, "w3_raw")
+        nc.sync.dma_start(w3_raw[:].bitcast(I32), w3_words[0].bitcast(I32))
+        xs = held([P, n_moor, S], U32, "xs")
+        nc.sync.dma_start(xs[:].bitcast(I32), xs_words.rearrange("a p n i -> p a (n i)").bitcast(I32))
+        for q in range(QUADS):
+            nc.sync.dma_start(
+                tab_sc[32 * q:32 * q + 4 * n_sea, :].bitcast(I32),
+                tab_scales[:, 4 * q:4 * q + 4, :].bitcast(I32),
+            )
+        w1_raw0 = load_rows(w1, 0, 0, H, "w1_raw0")
+        load_tab(2)
+        w1_raw1 = load_rows(w1, 1, 0, H, "w1_raw1")
+        w1_raw2a = load_rows(w1, 2, 0, H // 2, "w1_raw2a")
+        w1_raw2b = load_rows(w1, 2, H // 2, H, "w1_raw2b")
+        w2_rawa = load_rows(w2, 0, 0, H // 2, "w2_rawa")
+        w2_rawb = load_rows(w2, 0, H // 2, H, "w2_rawb")
+        load_planes(nc.gpsimd, wx_sc_raw, wx_scales)
+        load_planes(nc.gpsimd, w3_sc_raw, w3_scales)
+
+        def offs_of(h):
+            return offsets[:, h * (HALF // 16):(h + 1) * (HALF // 16)]
+
+        picked = {}
+
+        def gather_words(a):
+            for h in range(halves):
+                picked[a, h] = held([P, HALF], U32, f"picked{a}_{h}")
+                nc.vector.tensor_copy(picked[a, h][:], tab[a][:].indirect(offs_of(h)))
+
+        def round_views(grouped, raw, m0, m1, raw_m0):
+            dst = grouped[:].rearrange("p (t m j) -> p m j t", t=PACK, j=PACK)[:, m0:m1, :, :]
+            src = raw[:].rearrange("p j (m t) -> p m j t", t=PACK)[:, m0 - raw_m0:m1 - raw_m0, :, :]
+            return dst, src
+
+        def round_vector(grouped, raw, m0, m1, raw_m0):
+            dst, src = round_views(grouped, raw, m0, m1, raw_m0)
+            nc.vector.tensor_copy(dst, src)
+
+        def round_scalar(grouped, raw, m0, m1, raw_m0):
+            dst, src = round_views(grouped, raw, m0, m1, raw_m0)
+            nc.scalar.copy(dst, src)
+
+        def quantize(codes, scales, grouped):
+            nc.vector.quantize_mx(out=codes.bitcast(FP8X4), scales=scales, in_=grouped)
+
+        def weight_tiles(name):
+            return (held([P, PACK * H], BF16, name + "_bf"), held([P, H], U32, name + "_codes"),
+                    held([P, H], U8, name + "_sc"))
+
+        def dealt(ap):
+            return ap.rearrange("p (g t m) -> p g m t", t=PACK, m=P)
+
+        def undealt(ap):
+            return ap.rearrange("p (g m t) -> p g m t", t=PACK, m=P)
+
+        def cols(t):
+            return slice(t * P, (t + 1) * P)
+
+        def woven(grouped):
+            return grouped[:].rearrange("p (c i t) -> p c t i", i=4, t=PACK)
+
+        def unwoven(rows):
+            return rows[:].rearrange("p t (c i) -> p c t i", i=4)
+
+        gather_words(0)
+        gather_words(1)
+        w1_t = [weight_tiles(f"w1_{a}") for a in range(n_sea)]
+
+        picked_sc = []
+        for h in range(halves):
+            plane = held([P, HALF], U8, f"picked_sc{h}")
+            nc.vector.tensor_copy(plane[:], tab_sc[:].indirect(offs_of(h)))
+            picked_sc.append(plane)
+
+        wx = held([P, n_moor * H], U16, "wx")
+        nc.scalar.copy(dealt(wx[:]), undealt(wx_raw[:].rearrange("p a c -> p (a c)")))
+        wx_sc = held([P, n_moor * H], U8, "wx_sc")
+        nc.vector.tensor_copy(dealt(wx_sc[:]), undealt(wx_sc_raw[:].rearrange("p a c -> p (a c)")))
+
+        moor = {}
+        for h in range(halves):
+            for t in range(PACK):
+                acc = bank([P, HALF])
+                for a in range(n_moor):
+                    nc.tensor.matmul_mx(
+                        out=acc[:],
+                        lhsT=wx[:, cols(a * PACK + t)].bitcast(FP4X4),
+                        lhsT_scale=wx_sc[:, cols(a * PACK + t)],
+                        rhs=xs[:, a, h * HALF:(h + 1) * HALF].bitcast(FP8X4),
+                        rhs_scale=xs_sc[:, a, h * HALF:(h + 1) * HALF],
+                        start=(a == 0), stop=(a == n_moor - 1),
+                    )
+                moor[t, h] = held([P, HALF], F32, f"moor{t}_{h}")
+                nc.scalar.activation(moor[t, h][:], acc[:], ACT.Copy)
+
+        round_vector(w1_t[0][0], w1_raw0, 0, P, 0)
+        quantize(w1_t[0][1][:], w1_t[0][2][:], w1_t[0][0][:])
+        w3 = held([P, N], U16, "w3")
+        nc.scalar.copy(dealt(w3[:]), undealt(w3_raw[:]))
+        w3_sc = held([P, N], U8, "w3_sc")
+        nc.vector.tensor_copy(dealt(w3_sc[:]), undealt(w3_sc_raw[:, 0, :]))
+        gather_words(2)
+        round_vector(w1_t[1][0], w1_raw1, 0, 64, 0)
+        round_scalar(w1_t[1][0], w1_raw1, 64, P, 0)
+        quantize(w1_t[1][1][:], w1_t[1][2][:], w1_t[1][0][:])
+
+        sea = {}
+
+        def sea_pass(a, h, t):
+            nc.tensor.matmul_mx(
+                out=sea[t, h][:],
+                lhsT=w1_t[a][1][:, cols(t)].bitcast(FP8X4),
+                lhsT_scale=w1_t[a][2][:, cols(t)],
+                rhs=picked[a, h][:].bitcast(FP8X4),
+                rhs_scale=picked_sc[h][4 * a:P, :],
+                start=(a == 0), stop=(a == n_sea - 1),
+            )
+
+        for h in range(halves):
+            for t in range(PACK):
+                sea[t, h] = bank([P, HALF])
+                sea_pass(0, h, t)
+        round_scalar(w1_t[2][0], w1_raw2a, 0, 64, 0)
+        round_vector(w1_t[2][0], w1_raw2b, 64, 104, 64)
+        round_scalar(w1_t[2][0], w1_raw2b, 104, P, 64)
+        for u in range(2):
+            quantize(w1_t[2][1][:, u * 256:(u + 1) * 256], w1_t[2][2][:, u * 256:(u + 1) * 256],
+                     w1_t[2][0][:, u * 1024:(u + 1) * 1024])
+        for h in range(halves):
+            for a in range(1, n_sea):
+                for t in range(PACK):
+                    sea_pass(a, h, t)
+
+        w2_t = weight_tiles("w2")
+        round_scalar(w2_t[0], w2_rawa, 0, 64, 0)
+        round_scalar(w2_t[0], w2_rawb, 64, P, 64)
+
+        y_sc = held([P, n_groups, S], U8, "y_sc")
+
+        def in_half(c):
+            h, c0 = divmod(c * W, HALF)
+            return h, slice(c0, c0 + W)
+
+        z_bf, z_q, d_q = {}, {}, {}
+
+        def make_z(c):
+            h, cs = in_half(c)
+            rows = ring.tile([P, PACK, W], BF16, name="z_rows", align_bytes=64)
+            for t in range(PACK):
+                nc.vector.scalar_tensor_tensor(
+                    rows[:, t, :], sea[t, h][:, cs], b1[:, t:t + 1], moor[t, h][:, cs], ALU.add, ALU.max
+                )
+            z_bf[c] = held([P, PACK * W], BF16, f"z_bf{c}")
+            nc.scalar.copy(woven(z_bf[c]), unwoven(rows))
+
+        def quantize_z(c):
+            z_q[c] = (held([P, W], U32, f"z_codes{c}"), held([P, W], U8, f"z_sc{c}"))
+            quantize(z_q[c][0][:], z_q[c][1][:], z_bf[c][:])
+
+        th = {}
+
+        def respond(c):
+            th[c] = ring.tile([P, PACK, W], F32, name="th", bufs=3, align_bytes=64)
+            for u in range(2):
+                acc = bank([P, 2, W])
+                for e in range(2):
+                    t = 2 * u + e
+                    nc.tensor.matmul_mx(
+                        out=acc[:, e, :],
+                        lhsT=w2_t[1][:, cols(t)].bitcast(FP8X4), lhsT_scale=w2_t[2][:, cols(t)],
+                        rhs=z_q[c][0][:].bitcast(FP8X4), rhs_scale=z_q[c][1][:],
+                        start=True, stop=True,
+                    )
+                for e in range(2):
+                    t = 2 * u + e
+                    nc.scalar.activation(th[c][:, t, :], acc[:, e, :], ACT.Tanh, bias=b2[:, t:t + 1])
+
+        d_bf = {}
+
+        def make_diff(c):
+            h, cs = in_half(c)
+            rows = ring.tile([P, PACK, W], BF16, name="d_rows", align_bytes=64)
+            for t in range(PACK):
+                nc.vector.scalar_tensor_tensor(
+                    rows[:, t, :], th[c][:, t, :], gn[:, t:t + 1], moor[t, h][:, cs], ALU.mult, ALU.subtract
+                )
+            d_bf[c] = ring.tile([P, PACK * W], BF16, name="d_bf", align_bytes=64)
+            if c == 1:
+                nc.scalar.copy(woven(d_bf[c]), unwoven(rows))
+            else:
+                nc.vector.tensor_copy(woven(d_bf[c]), unwoven(rows))
+
+        def quantize_diff(c):
+            d_q[c] = (held([P, W], U32, f"d_codes{c}"), held([P, W], U8, f"d_sc{c}"))
+            quantize(d_q[c][0][:], d_q[c][1][:], d_bf[c][:])
+
+        y = {}
+
+        def make_y(c):
+            for g in range(n_groups):
+                y[g, c] = held([P, PACK, W], F32, f"y{g}_{c}")
+                for u in range(2):
+                    acc = bank([P, 2, W])
+                    for e in range(2):
+                        t = g * PACK + 2 * u + e
+                        nc.tensor.matmul_mx(
+                            out=acc[:, e, :],
+                            lhsT=w3[:, cols(t)].bitcast(FP4X4), lhsT_scale=w3_sc[:, cols(t)],
+                            rhs=d_q[c][0][:].bitcast(FP8X4), rhs_scale=d_q[c][1][:],
+                            start=True, stop=True,
+                        )
+                    nc.scalar.copy(y[g, c][:, 2 * u:2 * u + 2, :], acc[:])
+                nc.sync.dma_start(
+                    out_0[g * PASS:(g + 1) * PASS, c * W:(c + 1) * W].rearrange("(p t) m -> p t m", t=PACK),
+                    y[g, c][:],
+                )
+
+        def planes_of_y(c):
+            codes = held([P, n_groups, W], U32, f"y_codes{c}")
+            grouped = []
+            for g in range(n_groups):
+                y_bf = ring.tile([P, PACK * W], BF16, name="y_bf", align_bytes=64)
+                if (c, g) == (3, 1):
+                    nc.scalar.copy(woven(y_bf), unwoven(y[g, c]))
+                else:
+                    nc.vector.tensor_copy(woven(y_bf), unwoven(y[g, c]))
+                grouped.append(y_bf)
+            for g in range(n_groups):
+                quantize(codes[:, g, :], y_sc[:, g, c * W:(c + 1) * W], grouped[g][:])
+            nc.sync.dma_start(
+                out_1[:, :, c * W:(c + 1) * W, :].rearrange("g p m i -> p g (m i)").bitcast(I32),
+                codes[:].bitcast(I32),
+            )
+
+        make_z(0)
+        make_z(1)
+        quantize(w2_t[1][:], w2_t[2][:], w2_t[0][:])
+        quantize_z(0)
+        respond(0)
+        make_z(2)
+        quantize_z(1)
+        respond(1)
+        make_z(3)
+        make_diff(0)
+        quantize_diff(0)
+        quantize_z(2)
+        respond(2)
+        make_y(0)
+        make_diff(1)
+        quantize_diff(1)
+        quantize_z(3)
+        respond(3)
+        make_y(1)
+        make_diff(2)
+        quantize_diff(2)
+        planes_of_y(0)
+        make_y(2)
+        make_diff(3)
+        quantize_diff(3)
+        planes_of_y(1)
+        make_y(3)
+        planes_of_y(2)
+        planes_of_y(3)
+        for q in range(QUADS):
+            nc.sync.dma_start(
+                out_2[:, 4 * q:4 * q + 4, :].rearrange("g r m -> r g m").bitcast(I32),
+                y_sc[32 * q:32 * q + 4, :, :].bitcast(I32),
+            )

@@ -43,13 +43,12 @@ def tile_list_buoy_damping_features_kernel(
         def bank(shape):
             return psum.tile(shape, F32, name="bank")
 
-        wx_sc_raw = held([P, n_moor, H], U8, "wx_sc_raw")
+        wx_sc_raw = keep.tile([P, n_moor, H], U8, name="wx_sc_raw", tag="wx_sc_raw", align_bytes=64)
         xs_sc = held([P, n_moor, S], U8, "xs_sc")
-        tab_sc = held([P, T], U8, "tab_sc")
+        tab_sc = keep.tile([P, T], U8, name="tab_sc", tag="tab_sc", align_bytes=64)
         w3_sc_raw = held([P, 1, N], U8, "w3_sc_raw")
-        nc.vector.memset(tab_sc[:, :T // 2].bitcast(I32), 0)
-        nc.gpsimd.memset(tab_sc[:, T // 2:].bitcast(I32), 0)
-        nc.vector.memset(wx_sc_raw[:].bitcast(I32), 0)
+        nc.vector.memset(tab_sc[:].bitcast(I32), 0)
+        nc.gpsimd.memset(wx_sc_raw[:].bitcast(I32), 0)
         nc.vector.memset(w3_sc_raw[:].bitcast(I32), 0)
 
         offsets = keep.tile([P, S // 16], U16, name="offsets")
@@ -70,39 +69,39 @@ def tile_list_buoy_damping_features_kernel(
             nc.sync.dma_start(col[:], v.rearrange("(p t) -> p t", t=PACK))
             return col
 
-        def load_planes(queue, plane, scales):
+        def load_planes(plane, scales):
             for q in range(QUADS):
-                queue.dma_start(
+                nc.sync.dma_start(
                     plane[32 * q:32 * q + 4, :, :].bitcast(I32),
                     scales[:, 4 * q:4 * q + 4, :].rearrange("a r n -> r a n").bitcast(I32),
                 )
 
-        load_tab(0)
+        load_planes(xs_sc, xs_scales)
         wx_raw = held([P, n_moor, H], U16, "wx_raw")
         nc.sync.dma_start(wx_raw[:].bitcast(I32), wx_words.rearrange("a p b -> p a b").bitcast(I32))
-        load_planes(nc.sync, xs_sc, xs_scales)
-        load_tab(1)
-        b1 = load_vec(bias1, "b1")
-        b2 = load_vec(bias2, "b2")
-        gn = load_vec(gain, "gn")
-        w3_raw = held([P, N], U16, "w3_raw")
-        nc.sync.dma_start(w3_raw[:].bitcast(I32), w3_words[0].bitcast(I32))
-        xs = held([P, n_moor, S], U32, "xs")
-        nc.sync.dma_start(xs[:].bitcast(I32), xs_words.rearrange("a p n i -> p a (n i)").bitcast(I32))
+        load_tab(0)
+        w1_raw0 = load_rows(w1, 0, 0, H, "w1_raw0")
         for q in range(QUADS):
             nc.sync.dma_start(
                 tab_sc[32 * q:32 * q + 4 * n_sea, :].bitcast(I32),
                 tab_scales[:, 4 * q:4 * q + 4, :].bitcast(I32),
             )
-        w1_raw0 = load_rows(w1, 0, 0, H, "w1_raw0")
+        xs = held([P, n_moor, S], U32, "xs")
+        nc.sync.dma_start(xs[:].bitcast(I32), xs_words.rearrange("a p n i -> p a (n i)").bitcast(I32))
+        load_planes(wx_sc_raw, wx_scales)
+        load_tab(1)
         load_tab(2)
+        b1 = load_vec(bias1, "b1")
         w1_raw1 = load_rows(w1, 1, 0, H, "w1_raw1")
         w1_raw2a = load_rows(w1, 2, 0, H // 2, "w1_raw2a")
         w1_raw2b = load_rows(w1, 2, H // 2, H, "w1_raw2b")
         w2_rawa = load_rows(w2, 0, 0, H // 2, "w2_rawa")
         w2_rawb = load_rows(w2, 0, H // 2, H, "w2_rawb")
-        load_planes(nc.gpsimd, wx_sc_raw, wx_scales)
-        load_planes(nc.gpsimd, w3_sc_raw, w3_scales)
+        b2 = load_vec(bias2, "b2")
+        gn = load_vec(gain, "gn")
+        w3_raw = held([P, N], U16, "w3_raw")
+        nc.sync.dma_start(w3_raw[:].bitcast(I32), w3_words[0].bitcast(I32))
+        load_planes(w3_sc_raw, w3_scales)
 
         def offs_of(h):
             return offsets[:, h * (HALF // 16):(h + 1) * (HALF // 16)]
@@ -150,19 +149,18 @@ def tile_list_buoy_damping_features_kernel(
             return rows[:].rearrange("p t (c i) -> p c t i", i=4)
 
         gather_words(0)
-        gather_words(1)
-        w1_t = [weight_tiles(f"w1_{a}") for a in range(n_sea)]
+        w1_t = [(held([P, PACK * H], BF16, "w1_0_bf"),)] + [weight_tiles(f"w1_{a}") for a in range(1, n_sea)]
+
+        wx = held([P, n_moor * H], U16, "wx")
+        nc.scalar.copy(dealt(wx[:]), undealt(wx_raw[:].rearrange("p a c -> p (a c)")))
+        wx_sc = held([P, n_moor * H], U8, "wx_sc")
+        nc.vector.tensor_copy(dealt(wx_sc[:]), undealt(wx_sc_raw[:].rearrange("p a c -> p (a c)")))
 
         picked_sc = []
         for h in range(halves):
             plane = held([P, HALF], U8, f"picked_sc{h}")
             nc.vector.tensor_copy(plane[:], tab_sc[:].indirect(offs_of(h)))
             picked_sc.append(plane)
-
-        wx = held([P, n_moor * H], U16, "wx")
-        nc.scalar.copy(dealt(wx[:]), undealt(wx_raw[:].rearrange("p a c -> p (a c)")))
-        wx_sc = held([P, n_moor * H], U8, "wx_sc")
-        nc.vector.tensor_copy(dealt(wx_sc[:]), undealt(wx_sc_raw[:].rearrange("p a c -> p (a c)")))
 
         moor = {}
         for h in range(halves):
@@ -180,12 +178,14 @@ def tile_list_buoy_damping_features_kernel(
                 moor[t, h] = held([P, HALF], F32, f"moor{t}_{h}")
                 nc.scalar.activation(moor[t, h][:], acc[:], ACT.Copy)
 
-        round_vector(w1_t[0][0], w1_raw0, 0, P, 0)
+        round_scalar(w1_t[0][0], w1_raw0, 0, P, 0)
+        w1_t[0] = (
+            w1_t[0][0],
+            keep.tile([P, H], U32, name="w1_0_codes", tag="tab_sc", align_bytes=64),
+            keep.tile([P, H], U8, name="w1_0_sc", tag="wx_sc_raw", align_bytes=64),
+        )
         quantize(w1_t[0][1][:], w1_t[0][2][:], w1_t[0][0][:])
-        w3 = held([P, N], U16, "w3")
-        nc.scalar.copy(dealt(w3[:]), undealt(w3_raw[:]))
-        w3_sc = held([P, N], U8, "w3_sc")
-        nc.vector.tensor_copy(dealt(w3_sc[:]), undealt(w3_sc_raw[:, 0, :]))
+        gather_words(1)
         gather_words(2)
         round_vector(w1_t[1][0], w1_raw1, 0, 64, 0)
         round_scalar(w1_t[1][0], w1_raw1, 64, P, 0)
@@ -208,8 +208,7 @@ def tile_list_buoy_damping_features_kernel(
                 sea[t, h] = bank([P, HALF])
                 sea_pass(0, h, t)
         round_scalar(w1_t[2][0], w1_raw2a, 0, 64, 0)
-        round_vector(w1_t[2][0], w1_raw2b, 64, 104, 64)
-        round_scalar(w1_t[2][0], w1_raw2b, 104, P, 64)
+        round_vector(w1_t[2][0], w1_raw2b, 64, P, 64)
         for u in range(2):
             quantize(w1_t[2][1][:, u * 256:(u + 1) * 256], w1_t[2][2][:, u * 256:(u + 1) * 256],
                      w1_t[2][0][:, u * 1024:(u + 1) * 1024])
@@ -241,6 +240,8 @@ def tile_list_buoy_damping_features_kernel(
             nc.scalar.copy(woven(z_bf[c]), unwoven(rows))
 
         def quantize_z(c):
+            if c == 0:
+                quantize(w2_t[1][:], w2_t[2][:], w2_t[0][:])
             z_q[c] = (held([P, W], U32, f"z_codes{c}"), held([P, W], U8, f"z_sc{c}"))
             quantize(z_q[c][0][:], z_q[c][1][:], z_bf[c][:])
 
@@ -272,10 +273,7 @@ def tile_list_buoy_damping_features_kernel(
                     rows[:, t, :], th[c][:, t, :], gn[:, t:t + 1], moor[t, h][:, cs], ALU.mult, ALU.subtract
                 )
             d_bf[c] = ring.tile([P, PACK * W], BF16, name="d_bf", align_bytes=64)
-            if c == 1:
-                nc.scalar.copy(woven(d_bf[c]), unwoven(rows))
-            else:
-                nc.vector.tensor_copy(woven(d_bf[c]), unwoven(rows))
+            nc.vector.tensor_copy(woven(d_bf[c]), unwoven(rows))
 
         def quantize_diff(c):
             d_q[c] = (held([P, W], U32, f"d_codes{c}"), held([P, W], U8, f"d_sc{c}"))
@@ -319,35 +317,16 @@ def tile_list_buoy_damping_features_kernel(
                 codes[:].bitcast(I32),
             )
 
-        make_z(0)
-        make_z(1)
-        quantize(w2_t[1][:], w2_t[2][:], w2_t[0][:])
-        quantize_z(0)
-        respond(0)
-        make_z(2)
-        quantize_z(1)
-        respond(1)
-        make_z(3)
-        make_diff(0)
-        quantize_diff(0)
-        quantize_z(2)
-        respond(2)
-        make_y(0)
-        make_diff(1)
-        quantize_diff(1)
-        quantize_z(3)
-        respond(3)
-        make_y(1)
-        make_diff(2)
-        quantize_diff(2)
-        planes_of_y(0)
-        make_y(2)
-        make_diff(3)
-        quantize_diff(3)
-        planes_of_y(1)
-        make_y(3)
-        planes_of_y(2)
-        planes_of_y(3)
+        w3 = held([P, N], U16, "w3")
+        w3_sc = held([P, N], U8, "w3_sc")
+        stages = (make_z, quantize_z, respond, make_diff, quantize_diff, make_y, planes_of_y)
+        for step in range(chunks + len(stages) - 1):
+            if step == 4:
+                nc.scalar.copy(dealt(w3[:]), undealt(w3_raw[:]))
+                nc.vector.tensor_copy(dealt(w3_sc[:]), undealt(w3_sc_raw[:, 0, :]))
+            for lag, stage in enumerate(stages):
+                if 0 <= step - lag < chunks:
+                    stage(step - lag)
         for q in range(QUADS):
             nc.sync.dma_start(
                 out_2[:, 4 * q:4 * q + 4, :].rearrange("g r m -> r g m").bitcast(I32),

@@ -70,10 +70,10 @@ def tile_list_buoy_damping_features_kernel(
             return col
 
         def load_planes(plane, scales):
-            for q in range(QUADS):
+            for r in range(4):
                 nc.sync.dma_start(
-                    plane[32 * q:32 * q + 4, :, :].bitcast(I32),
-                    scales[:, 4 * q:4 * q + 4, :].rearrange("a r n -> r a n").bitcast(I32),
+                    plane[r:P:32, :, :].bitcast(I32),
+                    scales[:, r:16:4, :].rearrange("a q n -> q a n").bitcast(I32),
                 )
 
         load_planes(xs_sc, xs_scales)
@@ -91,6 +91,7 @@ def tile_list_buoy_damping_features_kernel(
         load_planes(wx_sc_raw, wx_scales)
         load_tab(1)
         load_tab(2)
+        load_planes(w3_sc_raw, w3_scales)
         b1 = load_vec(bias1, "b1")
         w1_raw1 = load_rows(w1, 1, 0, H, "w1_raw1")
         w1_raw2a = load_rows(w1, 2, 0, H // 2, "w1_raw2a")
@@ -101,7 +102,6 @@ def tile_list_buoy_damping_features_kernel(
         gn = load_vec(gain, "gn")
         w3_raw = held([P, N], U16, "w3_raw")
         nc.sync.dma_start(w3_raw[:].bitcast(I32), w3_words[0].bitcast(I32))
-        load_planes(w3_sc_raw, w3_scales)
 
         def offs_of(h):
             return offsets[:, h * (HALF // 16):(h + 1) * (HALF // 16)]
@@ -134,10 +134,10 @@ def tile_list_buoy_damping_features_kernel(
                     held([P, H], U8, name + "_sc"))
 
         def dealt(ap):
-            return ap.rearrange("p (g t m) -> p g m t", t=PACK, m=P)
+            return ap.rearrange("p (g t m) -> p g t m", t=PACK, m=P)
 
         def undealt(ap):
-            return ap.rearrange("p (g m t) -> p g m t", t=PACK, m=P)
+            return ap.rearrange("p (g m t) -> p g t m", t=PACK, m=P)
 
         def cols(t):
             return slice(t * P, (t + 1) * P)
@@ -187,6 +187,8 @@ def tile_list_buoy_damping_features_kernel(
         quantize(w1_t[0][1][:], w1_t[0][2][:], w1_t[0][0][:])
         gather_words(1)
         gather_words(2)
+        w3_sc = held([P, N], U8, "w3_sc")
+        nc.vector.tensor_copy(dealt(w3_sc[:]), undealt(w3_sc_raw[:, 0, :]))
         round_vector(w1_t[1][0], w1_raw1, 0, 64, 0)
         round_scalar(w1_t[1][0], w1_raw1, 64, P, 0)
         quantize(w1_t[1][1][:], w1_t[1][2][:], w1_t[1][0][:])
@@ -316,19 +318,19 @@ def tile_list_buoy_damping_features_kernel(
                 out_1[:, :, c * W:(c + 1) * W, :].rearrange("g p m i -> p g (m i)").bitcast(I32),
                 codes[:].bitcast(I32),
             )
+            if (c + 1) * W % HALF == 0:
+                span = slice((c + 1) * W - HALF, (c + 1) * W)
+                for r in range(4):
+                    nc.sync.dma_start(
+                        out_2[:, r:16:4, span].rearrange("g q m -> q g m").bitcast(I32),
+                        y_sc[r:P:32, :, span].bitcast(I32),
+                    )
 
         w3 = held([P, N], U16, "w3")
-        w3_sc = held([P, N], U8, "w3_sc")
         stages = (make_z, quantize_z, respond, make_diff, quantize_diff, make_y, planes_of_y)
         for step in range(chunks + len(stages) - 1):
             if step == 4:
                 nc.scalar.copy(dealt(w3[:]), undealt(w3_raw[:]))
-                nc.vector.tensor_copy(dealt(w3_sc[:]), undealt(w3_sc_raw[:, 0, :]))
             for lag, stage in enumerate(stages):
                 if 0 <= step - lag < chunks:
                     stage(step - lag)
-        for q in range(QUADS):
-            nc.sync.dma_start(
-                out_2[:, 4 * q:4 * q + 4, :].rearrange("g r m -> r g m").bitcast(I32),
-                y_sc[32 * q:32 * q + 4, :, :].bitcast(I32),
-            )

@@ -76,19 +76,19 @@ def tile_list_buoy_damping_features_kernel(
                     scales[:, r:16:4, :].rearrange("a q n -> q a n").bitcast(I32),
                 )
 
+        load_tab(0)
         load_planes(xs_sc, xs_scales)
         wx_raw = held([P, n_moor, H], U16, "wx_raw")
         nc.sync.dma_start(wx_raw[:].bitcast(I32), wx_words.rearrange("a p b -> p a b").bitcast(I32))
-        load_tab(0)
         w1_raw0 = load_rows(w1, 0, 0, H, "w1_raw0")
         for q in range(QUADS):
-            nc.sync.dma_start(
+            nc.gpsimd.dma_start(
                 tab_sc[32 * q:32 * q + 4 * n_sea, :].bitcast(I32),
                 tab_scales[:, 4 * q:4 * q + 4, :].bitcast(I32),
             )
+        load_planes(wx_sc_raw, wx_scales)
         xs = held([P, n_moor, S], U32, "xs")
         nc.sync.dma_start(xs[:].bitcast(I32), xs_words.rearrange("a p n i -> p a (n i)").bitcast(I32))
-        load_planes(wx_sc_raw, wx_scales)
         load_tab(1)
         load_tab(2)
         load_planes(w3_sc_raw, w3_scales)
@@ -156,11 +156,8 @@ def tile_list_buoy_damping_features_kernel(
         wx_sc = held([P, n_moor * H], U8, "wx_sc")
         nc.vector.tensor_copy(dealt(wx_sc[:]), undealt(wx_sc_raw[:].rearrange("p a c -> p (a c)")))
 
-        picked_sc = []
-        for h in range(halves):
-            plane = held([P, HALF], U8, f"picked_sc{h}")
-            nc.vector.tensor_copy(plane[:], tab_sc[:].indirect(offs_of(h)))
-            picked_sc.append(plane)
+        picked_sc = keep.tile([P, S], U8, name="picked_sc", tag="wx_sc_raw", align_bytes=64)
+        nc.vector.tensor_copy(picked_sc[:], tab_sc[:].indirect(offsets[:]))
 
         moor = {}
         for h in range(halves):
@@ -182,7 +179,7 @@ def tile_list_buoy_damping_features_kernel(
         w1_t[0] = (
             w1_t[0][0],
             keep.tile([P, H], U32, name="w1_0_codes", tag="tab_sc", align_bytes=64),
-            keep.tile([P, H], U8, name="w1_0_sc", tag="wx_sc_raw", align_bytes=64),
+            held([P, H], U8, "w1_0_sc"),
         )
         quantize(w1_t[0][1][:], w1_t[0][2][:], w1_t[0][0][:])
         gather_words(1)
@@ -201,7 +198,7 @@ def tile_list_buoy_damping_features_kernel(
                 lhsT=w1_t[a][1][:, cols(t)].bitcast(FP8X4),
                 lhsT_scale=w1_t[a][2][:, cols(t)],
                 rhs=picked[a, h][:].bitcast(FP8X4),
-                rhs_scale=picked_sc[h][4 * a:P, :],
+                rhs_scale=picked_sc[4 * a:P, h * HALF:(h + 1) * HALF],
                 start=(a == 0), stop=(a == n_sea - 1),
             )
 

from contextlib import ExitStack

import concourse.mybir as mybir

K, K2, T, S, H, N = 1536, 1024, 2048, 1024, 512, 1024
FLOPS = 2 * S * (K * H + K2 * H + H * H + H * N)

F32 = mybir.dt.float32
BF16 = mybir.dt.bfloat16
I32 = mybir.dt.int32
U32 = mybir.dt.uint32
U16 = mybir.dt.uint16
U8 = mybir.dt.uint8
FP8X4 = mybir.dt.float8_e4m3fn_x4
FP4X4 = mybir.dt.float4_e2m1fn_x4
ALU = mybir.AluOpType
ACT = mybir.ActivationFunctionType

P = 128
PACK = 4
PASS = P * PACK
HALF = 512
W = 256
QUADS = 4


def tile_list_buoy_damping_features_kernel(
    tc, tab_words, tab_scales, offs, xs_words, xs_scales, w1, bias1, wx_words, wx_scales,
    w2, bias2, gain, w3_words, w3_scales, out_0, out_1, out_2,
):
    nc = tc.nc
    n_sea, n_moor, n_groups = K // PASS, K2 // PASS, N // PASS
    halves, chunks = S // HALF, S // W

    with ExitStack() as ctx:
        keep = ctx.enter_context(tc.tile_pool(name="keep", bufs=1))
        ring = ctx.enter_context(tc.tile_pool(name="ring", bufs=2))
        psum = ctx.enter_context(tc.psum_pool(name="psum", bufs=8))

        def held(shape, dtype, name):
            return keep.tile(shape, dtype, name=name, align_bytes=64)

        def bank(shape):
            return psum.tile(shape, F32, name="bank")

        wx_sc_raw = keep.tile([P, n_moor, H], U8, name="wx_sc_raw", tag="wx_sc_raw", align_bytes=64)
        xs_sc = held([P, n_moor, S], U8, "xs_sc")
        tab_sc = keep.tile([P, T], U8, name="tab_sc", tag="tab_sc", align_bytes=64)
        w3_sc_raw = held([P, 1, N], U8, "w3_sc_raw")
        nc.vector.memset(tab_sc[:].bitcast(I32), 0)
        nc.gpsimd.memset(wx_sc_raw[:].bitcast(I32), 0)
        nc.vector.memset(w3_sc_raw[:].bitcast(I32), 0)

        offsets = keep.tile([P, S // 16], U16, name="offsets")
        nc.sync.dma_start(offsets[:], offs)

        tab = [held([P, T], U32, f"tab{a}") for a in range(n_sea)]

        def load_tab(a):
            nc.sync.dma_start(tab[a][:].bitcast(I32), tab_words[a].rearrange("p n i -> p (n i)").bitcast(I32))

        def load_rows(w, a, c0, c1, name):
            raw = held([P, PACK, c1 - c0], F32, name)
            nc.sync.dma_start(raw[:], w[a * PASS:(a + 1) * PASS, c0:c1].rearrange("(p j) c -> p j c", j=PACK))
            return raw

        def load_vec(v, name):
            col = held([P, PACK], F32, name)
            nc.sync.dma_start(col[:], v.rearrange("(p t) -> p t", t=PACK))
            return col

        def load_planes(plane, scales):
            for r in range(4):
                nc.sync.dma_start(
                    plane[r:P:32, :, :].bitcast(I32),
                    scales[:, r:16:4, :].rearrange("a q n -> q a n").bitcast(I32),
                )

        load_tab(0)
        load_planes(xs_sc, xs_scales)
        wx_raw = held([P, n_moor, H], U16, "wx_raw")
        nc.sync.dma_start(wx_raw[:].bitcast(I32), wx_words.rearrange("a p b -> p a b").bitcast(I32))
        w1_raw0 = load_rows(w1, 0, 0, H, "w1_raw0")
        for q in range(QUADS):
            nc.gpsimd.dma_start(
                tab_sc[32 * q:32 * q + 4 * n_sea, :].bitcast(I32),
                tab_scales[:, 4 * q:4 * q + 4, :].bitcast(I32),
            )
        load_planes(wx_sc_raw, wx_scales)
        xs = held([P, n_moor, S], U32, "xs")
        nc.sync.dma_start(xs[:].bitcast(I32), xs_words.rearrange("a p n i -> p a (n i)").bitcast(I32))
        load_tab(1)
        load_tab(2)
        load_planes(w3_sc_raw, w3_scales)
        b1 = load_vec(bias1, "b1")
        w1_raw1 = load_rows(w1, 1, 0, H, "w1_raw1")
        w1_raw2a = load_rows(w1, 2, 0, H // 2, "w1_raw2a")
        w1_raw2b = load_rows(w1, 2, H // 2, H, "w1_raw2b")
        w2_rawa = load_rows(w2, 0, 0, H // 2, "w2_rawa")
        w2_rawb = load_rows(w2, 0, H // 2, H, "w2_rawb")
        b2 = load_vec(bias2, "b2")
        gn = load_vec(gain, "gn")
        w3_raw = held([P, N], U16, "w3_raw")
        nc.sync.dma_start(w3_raw[:].bitcast(I32), w3_words[0].bitcast(I32))

        def offs_of(h):
            return offsets[:, h * (HALF // 16):(h + 1) * (HALF // 16)]

        picked = {}

        def gather_words(a):
            for h in range(halves):
                picked[a, h] = held([P, HALF], U32, f"picked{a}_{h}")
                nc.vector.tensor_copy(picked[a, h][:], tab[a][:].indirect(offs_of(h)))

        def round_views(grouped, raw, m0, m1, raw_m0):
            dst = grouped[:].rearrange("p (t m j) -> p m j t", t=PACK, j=PACK)[:, m0:m1, :, :]
            src = raw[:].rearrange("p j (m t) -> p m j t", t=PACK)[:, m0 - raw_m0:m1 - raw_m0, :, :]
            return dst, src

        def round_vector(grouped, raw, m0, m1, raw_m0):
            dst, src = round_views(grouped, raw, m0, m1, raw_m0)
            nc.vector.tensor_copy(dst, src)

        def round_scalar(grouped, raw, m0, m1, raw_m0):
            dst, src = round_views(grouped, raw, m0, m1, raw_m0)
            nc.scalar.copy(dst, src)

        def quantize(codes, scales, grouped):
            nc.vector.quantize_mx(out=codes.bitcast(FP8X4), scales=scales, in_=grouped)

        def weight_tiles(name):
            return (held([P, PACK * H], BF16, name + "_bf"), held([P, H], U32, name + "_codes"),
                    held([P, H], U8, name + "_sc"))

        def dealt(ap):
            return ap.rearrange("p (g t m) -> p g t m", t=PACK, m=P)

        def undealt(ap):
            return ap.rearrange("p (g m t) -> p g t m", t=PACK, m=P)

        def cols(t):
            return slice(t * P, (t + 1) * P)

        def woven(grouped):
            return grouped[:].rearrange("p (c i t) -> p c t i", i=4, t=PACK)

        def unwoven(rows):
            return rows[:].rearrange("p t (c i) -> p c t i", i=4)

        gather_words(0)
        w1_t = [(held([P, PACK * H], BF16, "w1_0_bf"),)] + [weight_tiles(f"w1_{a}") for a in range(1, n_sea)]

        wx = held([P, n_moor * H], U16, "wx")
        nc.scalar.copy(dealt(wx[:]), undealt(wx_raw[:].rearrange("p a c -> p (a c)")))
        wx_sc = held([P, n_moor * H], U8, "wx_sc")
        nc.vector.tensor_copy(dealt(wx_sc[:]), undealt(wx_sc_raw[:].rearrange("p a c -> p (a c)")))

        picked_sc = keep.tile([P, S], U8, name="picked_sc", tag="wx_sc_raw", align_bytes=64)
        nc.vector.tensor_copy(picked_sc[:], tab_sc[:].indirect(offsets[:]))

        moor = {}
        for h in range(halves):
            for t in range(PACK):
                acc = bank([P, HALF])
                for a in range(n_moor):
                    nc.tensor.matmul_mx(
                        out=acc[:],
                        lhsT=wx[:, cols(a * PACK + t)].bitcast(FP4X4),
                        lhsT_scale=wx_sc[:, cols(a * PACK + t)],
                        rhs=xs[:, a, h * HALF:(h + 1) * HALF].bitcast(FP8X4),
                        rhs_scale=xs_sc[:, a, h * HALF:(h + 1) * HALF],
                        start=(a == 0), stop=(a == n_moor - 1),
                    )
                moor[t, h] = held([P, HALF], F32, f"moor{t}_{h}")
                nc.scalar.activation(moor[t, h][:], acc[:], ACT.Copy)

        round_scalar(w1_t[0][0], w1_raw0, 0, P, 0)
        w1_t[0] = (
            w1_t[0][0],
            keep.tile([P, H], U32, name="w1_0_codes", tag="tab_sc", align_bytes=64),
            held([P, H], U8, "w1_0_sc"),
        )
        quantize(w1_t[0][1][:], w1_t[0][2][:], w1_t[0][0][:])
        gather_words(1)
        gather_words(2)
        w3_sc = held([P, N], U8, "w3_sc")
        nc.vector.tensor_copy(dealt(w3_sc[:]), undealt(w3_sc_raw[:, 0, :]))
        round_vector(w1_t[1][0], w1_raw1, 0, 64, 0)
        round_scalar(w1_t[1][0], w1_raw1, 64, P, 0)
        quantize(w1_t[1][1][:], w1_t[1][2][:], w1_t[1][0][:])

        sea = {}

        def sea_pass(a, h, t):
            nc.tensor.matmul_mx(
                out=sea[t, h][:],
                lhsT=w1_t[a][1][:, cols(t)].bitcast(FP8X4),
                lhsT_scale=w1_t[a][2][:, cols(t)],
                rhs=picked[a, h][:].bitcast(FP8X4),
                rhs_scale=picked_sc[4 * a:P, h * HALF:(h + 1) * HALF],
                start=(a == 0), stop=(a == n_sea - 1),
            )

        for h in range(halves):
            for t in range(PACK):
                sea[t, h] = bank([P, HALF])
                sea_pass(0, h, t)
        round_scalar(w1_t[2][0], w1_raw2a, 0, 64, 0)
        round_vector(w1_t[2][0], w1_raw2b, 64, P, 64)
        for u in range(2):
            quantize(w1_t[2][1][:, u * 256:(u + 1) * 256], w1_t[2][2][:, u * 256:(u + 1) * 256],
                     w1_t[2][0][:, u * 1024:(u + 1) * 1024])
        for h in range(halves):
            for a in range(1, n_sea):
                for t in range(PACK):
                    sea_pass(a, h, t)

        w2_t = weight_tiles("w2")
        round_scalar(w2_t[0], w2_rawa, 0, 64, 0)
        round_scalar(w2_t[0], w2_rawb, 64, P, 64)

        y_sc = held([P, n_groups, S], U8, "y_sc")

        def in_half(c):
            h, c0 = divmod(c * W, HALF)
            return h, slice(c0, c0 + W)

        z_bf, z_q, d_q = {}, {}, {}

        def make_z(c):
            h, cs = in_half(c)
            rows = ring.tile([P, PACK, W], BF16, name="z_rows", align_bytes=64)
            for t in range(PACK):
                nc.vector.scalar_tensor_tensor(
                    rows[:, t, :], sea[t, h][:, cs], b1[:, t:t + 1], moor[t, h][:, cs], ALU.add, ALU.max
                )
            z_bf[c] = held([P, PACK * W], BF16, f"z_bf{c}")
            nc.scalar.copy(woven(z_bf[c]), unwoven(rows))

        def quantize_z(c):
            if c == 0:
                quantize(w2_t[1][:], w2_t[2][:], w2_t[0][:])
            z_q[c] = (held([P, W], U32, f"z_codes{c}"), held([P, W], U8, f"z_sc{c}"))
            quantize(z_q[c][0][:], z_q[c][1][:], z_bf[c][:])

        th = {}

        def respond(c):
            th[c] = ring.tile([P, PACK, W], F32, name="th", bufs=3, align_bytes=64)
            for u in range(2):
                acc = bank([P, 2, W])
                for e in range(2):
                    t = 2 * u + e
                    nc.tensor.matmul_mx(
                        out=acc[:, e, :],
                        lhsT=w2_t[1][:, cols(t)].bitcast(FP8X4), lhsT_scale=w2_t[2][:, cols(t)],
                        rhs=z_q[c][0][:].bitcast(FP8X4), rhs_scale=z_q[c][1][:],
                        start=True, stop=True,
                    )
                for e in range(2):
                    t = 2 * u + e
                    nc.scalar.activation(th[c][:, t, :], acc[:, e, :], ACT.Tanh, bias=b2[:, t:t + 1])

        d_bf = {}

        def make_diff(c):
            h, cs = in_half(c)
            rows = ring.tile([P, PACK, W], BF16, name="d_rows", align_bytes=64)
            for t in range(PACK):
                nc.vector.scalar_tensor_tensor(
                    rows[:, t, :], th[c][:, t, :], gn[:, t:t + 1], moor[t, h][:, cs], ALU.mult, ALU.subtract
                )
            d_bf[c] = ring.tile([P, PACK * W], BF16, name="d_bf", align_bytes=64)
            nc.vector.tensor_copy(woven(d_bf[c]), unwoven(rows))

        def quantize_diff(c):
            d_q[c] = (held([P, W], U32, f"d_codes{c}"), held([P, W], U8, f"d_sc{c}"))
            quantize(d_q[c][0][:], d_q[c][1][:], d_bf[c][:])

        y = {}

        def make_y(c):
            for g in range(n_groups):
                y[g, c] = held([P, PACK, W], F32, f"y{g}_{c}")
                for u in range(2):
                    acc = bank([P, 2, W])
                    for e in range(2):
                        t = g * PACK + 2 * u + e
                        nc.tensor.matmul_mx(
                            out=acc[:, e, :],
                            lhsT=w3[:, cols(t)].bitcast(FP4X4), lhsT_scale=w3_sc[:, cols(t)],
                            rhs=d_q[c][0][:].bitcast(FP8X4), rhs_scale=d_q[c][1][:],
                            start=True, stop=True,
                        )
                    nc.scalar.copy(y[g, c][:, 2 * u:2 * u + 2, :], acc[:])
                nc.sync.dma_start(
                    out_0[g * PASS:(g + 1) * PASS, c * W:(c + 1) * W].rearrange("(p t) m -> p t m", t=PACK),
                    y[g, c][:],
                )

        def planes_of_y(c):
            codes = held([P, n_groups, W], U32, f"y_codes{c}")
            grouped = []
            for g in range(n_groups):
                y_bf = ring.tile([P, PACK * W], BF16, name="y_bf", align_bytes=64)
                if (c, g) == (3, 1):
                    nc.scalar.copy(woven(y_bf), unwoven(y[g, c]))
                else:
                    nc.vector.tensor_copy(woven(y_bf), unwoven(y[g, c]))
                grouped.append(y_bf)
            for g in range(n_groups):
                quantize(codes[:, g, :], y_sc[:, g, c * W:(c + 1) * W], grouped[g][:])
            nc.sync.dma_start(
                out_1[:, :, c * W:(c + 1) * W, :].rearrange("g p m i -> p g (m i)").bitcast(I32),
                codes[:].bitcast(I32),
            )
            if (c + 1) * W % HALF == 0:
                span = slice((c + 1) * W - HALF, (c + 1) * W)
                for r in range(4):
                    nc.sync.dma_start(
                        out_2[:, r:16:4, span].rearrange("g q m -> q g m").bitcast(I32),
                        y_sc[r:P:32, :, span].bitcast(I32),
                    )

        w3 = held([P, N], U16, "w3")
        stages = (make_z, quantize_z, respond, make_diff, quantize_diff, make_y, planes_of_y)
        for step in range(chunks + len(stages) - 1):
            if step == 4:
                nc.scalar.copy(dealt(w3[:]), undealt(w3_raw[:]))
            for lag, stage in enumerate(stages):
                if 0 <= step - lag < chunks:
                    stage(step - lag)
